import numpy as np
import ml_dtypes


def mxq(x, axis, fmt="e4m3"):
    dtype, down = {"e4m3": (ml_dtypes.float8_e4m3fn, 7), "e5m2": (ml_dtypes.float8_e5m2, 14)}[fmt]
    v = np.moveaxis(np.asarray(x, np.float32).astype(ml_dtypes.bfloat16).astype(np.float64), axis, -1)
    blocks = v.reshape(v.shape[:-1] + (-1, 32))
    amax = np.abs(blocks).max(-1, keepdims=True)
    byte = np.maximum(np.where(amax > 0, np.frexp(amax)[1] - 1 + 127, 0) - down, 1)
    scale = np.exp2(byte - 127.0)
    codes = (blocks / scale).astype(np.float32).astype(dtype).astype(np.float64)
    return np.moveaxis((codes * scale).reshape(v.shape), -1, axis)


WIDE = False


def mx_kscale(k, group=512):
    if not WIDE:
        return np.ones(k)
    levels = np.array([10, -10, 5, -5, 0])
    if group != 512:
        return np.exp2(np.random.permutation(np.resize(levels, k // group))).repeat(group)
    if k % 512:
        return np.exp2(np.random.permutation(np.resize(levels, k // 32))).repeat(32)
    a = np.empty((k // 512, 16))
    for p in range(k // 512):
        a[p, :8] = np.random.permutation(np.resize(levels, 8))
        for g in range(8):
            far = levels[np.abs(levels - a[p, g]) >= 10]
            a[p, g + 8] = far[np.random.randint(len(far))]
    return np.exp2(a.ravel()).repeat(32)


def f64(x):
    return np.asarray(x).astype(np.float64)


def striped(idx):
    return np.tile(np.asarray(idx).reshape(-1, 16).T, (8, 1)).astype(np.uint16)


def unstriped(offs):
    return offs[:16].T.reshape(-1).astype(np.int64)


H, KV, D, NQ, N = 4, 1, 128, 512, 512


def setup_inputs():
    n = np.random.standard_normal
    s = mx_kscale(D, 0)[:, None]
    u = mx_kscale(N)
    t = np.random.uniform(0.5, 2.0, N) * u
    v = n((KV, N, 128))
    return {
        "qT": (n((H, D, NQ)) * s * (0.70 / np.sqrt(D))).astype(np.float32),
        "kT": (n((KV, D, N)) / s).astype(np.float32),
        "t": t.reshape(N, 1).astype(np.float32),
        "v": (v / t[:, None]).astype(np.float32),
        "gn": np.tile(np.random.uniform(0.5, 2.0, 128), (128, 1)).astype(np.float32),
    }


def reference(qT, kT, t, v, gn):
    a = np.repeat(mxq(f64(kT), 1, "e4m3"), H // KV, 0).transpose(0, 2, 1) @ mxq(f64(qT), 1, "e4m3")
    p = 1.0 / (1.0 + np.exp(-a))
    w = p * f64(t)
    y = mxq(w, 1, "e4m3").transpose(0, 2, 1) @ np.repeat(mxq(f64(v), 1, "e4m3"), H // KV, 0)
    y = y / 16.0
    y = y / np.sqrt(np.mean(np.square(y), -1, keepdims=True) + 1e-5) * f64(gn)[:1]
    return y

@@ -1,0 +1,197 @@
+from contextlib import ExitStack
+
+import concourse.mybir as mybir
+
+F32 = mybir.dt.float32
+BF16 = mybir.dt.bfloat16
+U32 = mybir.dt.uint32
+U8 = mybir.dt.uint8
+FP8X4 = mybir.dt.float8_e4m3fn_x4
+ACT = mybir.ActivationFunctionType
+ALU = mybir.AluOpType
+
+H, D, NQ, N, E = 4, 128, 512, 512, 128
+FLOPS = 2 * H * N * NQ * D + 2 * H * NQ * N * E
+
+P = 128
+PACK = 4
+ROWS = D // PACK
+CHUNKS = 2
+CHUNK_Q = NQ // CHUNKS
+BLOCKS = CHUNK_Q // P
+STEPS = CHUNKS * BLOCKS * H
+CHUNK_STEPS = BLOCKS * H
+MULT_LAG = 2
+SQUARE_LAG = 5
+
+
+def tile_rows_a_sigmoid_onorm_kernel(tc, qT, kT, t, v, gn, out):
+    nc = tc.nc
+    with ExitStack() as ctx:
+        sb = ctx.enter_context(tc.tile_pool(name="sb", bufs=1))
+        ps = ctx.enter_context(tc.psum_pool(name="ps", bufs=1))
+        ctx.enter_context(tc.manual_schedule())
+
+        def quantize(name, values):
+            words = values.shape[1] // PACK
+            codes = sb.tile([P, words], U32, name=name + "_codes", align_bytes=64)
+            scales = sb.tile([P, words], U8, name=name + "_scales", align_bytes=64)
+            nc.vector.quantize_mx(out=codes[:].bitcast(FP8X4), scales=scales[:], in_=values)
+            return codes, scales
+
+        k_raw = sb.tile([P, PACK, N], F32, name="k_raw")
+        k_rows = kT[0].rearrange("(p j) n -> p j n", j=PACK)
+        for g in range(H):
+            queue = nc.sync if g < 2 else nc.scalar
+            queue.dma_start(out=k_raw[ROWS * g : ROWS * (g + 1)], in_=k_rows)
+        q_rows = qT.rearrange("h (p j) n -> (h p) j n", j=PACK)
+        q_raw = [sb.tile([P, PACK, CHUNK_Q], F32, name="q_raw%d" % c) for c in range(CHUNKS)]
+        nc.sync.dma_start(out=q_raw[0][:], in_=q_rows[:, :, 0:CHUNK_Q])
+        v_raw = sb.tile([P, PACK, E], F32, name="v_raw")
+        nc.sync.dma_start(out=v_raw[:], in_=v[0].rearrange("(p j) e -> p j e", j=PACK))
+        t_sb = sb.tile([P, PACK], F32, name="t_sb")
+        nc.sync.dma_start(out=t_sb[:], in_=t.rearrange("(p j) o -> p (j o)", j=PACK))
+        nc.sync.dma_start(out=q_raw[1][:], in_=q_rows[:, :, CHUNK_Q:NQ])
+        gn_sb = sb.tile([P, E], F32, name="gn_sb")
+        nc.sync.dma_start(out=gn_sb[:], in_=gn)
+
+        warm_in = sb.tile([P, 8], F32, name="warm_in")
+        warm_out = sb.tile([P, 8], F32, name="warm_out")
+        nc.gpsimd.memset(warm_in[:], 0.0)
+        nc.scalar.activation(out=warm_out[:], in_=warm_in[:], func=ACT.Sigmoid)
+
+        k_dealt = k_raw[:].rearrange("p j (s r) -> p s j r", r=PACK)
+        k_bf = [sb.tile([P, 2, P, PACK], BF16, name="k_bf%d" % a, align_bytes=64) for a in range(2)]
+        nc.vector.tensor_copy(out=k_bf[0][:].rearrange("p r s j -> p s j r"), in_=k_dealt[:, :, :, 0:2])
+        nc.scalar.copy(out=k_bf[1][:].rearrange("p r s j -> p s j r"), in_=k_dealt[:, :, :, 2:4])
+
+        q_bf = [sb.tile([P, BLOCKS, P, PACK], BF16, name="q_bf%d" % c, align_bytes=64) for c in range(CHUNKS)]
+
+        def cast_queries(c):
+            nc.vector.tensor_copy(
+                out=q_bf[c][:].rearrange("p m s j -> p s j m"),
+                in_=q_raw[c][:].rearrange("p j (s m) -> p s j m", m=BLOCKS),
+            )
+
+        def quantize_queries(c):
+            return quantize("q%d" % c, q_bf[c][:].rearrange("p m s j -> p (m s j)"))
+
+        cast_queries(0)
+        k_mx = [quantize("k0", k_bf[0][:].rearrange("p r s j -> p (r s j)"))]
+        q_mx = [quantize_queries(0)]
+        v_bf = sb.tile([P, E, PACK], BF16, name="v_bf", align_bytes=64)
+        nc.vector.tensor_copy(
+            out=v_bf[:].rearrange("p (c i) j -> p c j i", i=4),
+            in_=v_raw[:].rearrange("p j (c i) -> p c j i", i=4),
+        )
+        k_mx.append(quantize("k1", k_bf[1][:].rearrange("p r s j -> p (r s j)")))
+        v_codes, v_scales = quantize("v", v_bf[:].rearrange("p e j -> p (e j)"))
+        cast_queries(1)
+
+        score_bank = [ps.tile([P, PACK, P], F32, name="score%d" % g) for g in range(H)]
+        y_bank = [ps.tile([P, 4, E], F32, name="y%d" % b) for b in range(4)]
+        sumsq = [sb.tile([P, CHUNK_STEPS], F32, name="sumsq%d" % c) for c in range(CHUNKS)]
+        rstd = [sb.tile([P, CHUNK_STEPS], F32, name="rstd%d" % c) for c in range(CHUNKS)]
+        squares = sb.tile([P, E], F32, name="squares")
+        t_words = t_sb[:, 0:PACK].unsqueeze(1).to_broadcast([P, P, PACK])
+        probs = {}
+        w_bf = {}
+
+        def y_of(i):
+            c, rest = divmod(i, CHUNK_STEPS)
+            return y_bank[2 * c + rest % 2][:, rest // 2, :]
+
+        def scores(i):
+            c, rest = divmod(i, CHUNK_STEPS)
+            m, g = divmod(rest, H)
+            rows = slice(ROWS * g, ROWS * (g + 1))
+            q_codes, q_scales = q_mx[c]
+            q_cols = slice(P * m, P * (m + 1))
+            for r in range(PACK):
+                k_codes, k_scales = k_mx[r // 2]
+                k_cols = slice(P * (r % 2), P * (r % 2 + 1))
+                nc.tensor.matmul_mx(
+                    out=score_bank[g][:, r, :],
+                    lhsT=k_codes[rows, k_cols].bitcast(FP8X4),
+                    lhsT_scale=k_scales[rows, k_cols],
+                    rhs=q_codes[rows, q_cols].bitcast(FP8X4),
+                    rhs_scale=q_scales[rows, q_cols],
+                    start=True,
+                    stop=True,
+                )
+
+        def sigmoid(i):
+            probs[i] = sb.tile([P, P, PACK], F32, name="probs%d" % i)
+            nc.scalar.activation(
+                out=probs[i][:], in_=score_bank[i % H][:].rearrange("p r n -> p n r"), func=ACT.Sigmoid
+            )
+
+        def weigh(i):
+            w_bf[i] = sb.tile([P, P, PACK], BF16, name="w_bf%d" % i, align_bytes=64)
+            nc.vector.tensor_tensor(out=w_bf[i][:], in0=probs[i][:], in1=t_words, op=ALU.mult)
+
+        def values(i):
+            w_codes, w_scales = quantize("w%d" % i, w_bf[i][:].rearrange("p n r -> p (n r)"))
+            nc.tensor.matmul_mx(
+                out=y_of(i),
+                lhsT=w_codes[:].bitcast(FP8X4),
+                lhsT_scale=w_scales[:],
+                rhs=v_codes[:].bitcast(FP8X4),
+                rhs_scale=v_scales[:],
+                start=True,
+                stop=True,
+            )
+
+        def sum_squares(i):
+            c, rest = divmod(i, CHUNK_STEPS)
+            nc.scalar.activation(
+                out=squares[:], in_=y_of(i), func=ACT.Square, accum_out=sumsq[c][:, rest : rest + 1]
+            )
+
+        def inverse_rms(c):
+            nc.scalar.activation(
+                out=rstd[c][:], in_=sumsq[c][:], func=ACT.Abs_reciprocal_sqrt, scale=1.0 / E, bias=256 * 1e-5
+            )
+
+        def normalise_and_store(c):
+            for pair in range(H // 2):
+                result = sb.tile([P, 2, BLOCKS, E], F32, name="result%d_%d" % (c, pair))
+                for hh in range(2):
+                    for m in range(BLOCKS):
+                        rest = H * m + 2 * pair + hh
+                        nc.vector.scalar_tensor_tensor(
+                            out=result[:, hh, m, :],
+                            in0=y_of(CHUNK_STEPS * c + rest),
+                            scalar=rstd[c][:, rest : rest + 1],
+                            in1=gn_sb[:],
+                            op0=ALU.mult,
+                            op1=ALU.mult,
+                        )
+                dst = out[2 * pair : 2 * pair + 2, CHUNK_Q * c : CHUNK_Q * (c + 1), :]
+                nc.sync.dma_start(
+                    out=dst.rearrange("h (s m) e -> s h (m e)", m=BLOCKS),
+                    in_=result[:].rearrange("p h m e -> p h (m e)"),
+                )
+
+        for i in range(H):
+            scores(i)
+        for i in range(STEPS + MULT_LAG + 1):
+            if i < STEPS:
+                sigmoid(i)
+                if i >= SQUARE_LAG:
+                    sum_squares(i - SQUARE_LAG)
+                if i + H < STEPS:
+                    scores(i + H)
+            if i == STEPS:
+                inverse_rms(0)
+            if MULT_LAG <= i < STEPS + MULT_LAG:
+                weigh(i - MULT_LAG)
+            if i == MULT_LAG:
+                q_mx.append(quantize_queries(1))
+            if i > MULT_LAG:
+                values(i - MULT_LAG - 1)
+        for i in range(STEPS - SQUARE_LAG, STEPS):
+            sum_squares(i)
+        normalise_and_store(0)
+        inverse_rms(1)
+        normalise_and_store(1)

@@ -79,63 +79,80 @@ def tile_rows_a_sigmoid_onorm_kernel(tc, qT, kT, t, v, gn, out):
         cast_queries(0)
         k_mx = [quantize("k0", k_bf[0][:].rearrange("p r s j -> p (r s j)"))]
         q_mx = [quantize_queries(0)]
+        k_mx.append(quantize("k1", k_bf[1][:].rearrange("p r s j -> p (r s j)")))
         v_bf = sb.tile([P, E, PACK], BF16, name="v_bf", align_bytes=64)
         nc.vector.tensor_copy(
             out=v_bf[:].rearrange("p (c i) j -> p c j i", i=4),
             in_=v_raw[:].rearrange("p j (c i) -> p c j i", i=4),
         )
-        k_mx.append(quantize("k1", k_bf[1][:].rearrange("p r s j -> p (r s j)")))
-        v_codes, v_scales = quantize("v", v_bf[:].rearrange("p e j -> p (e j)"))
         cast_queries(1)
+        v_codes, v_scales = quantize("v", v_bf[:].rearrange("p e j -> p (e j)"))
 
         score_bank = [ps.tile([P, PACK, P], F32, name="score%d" % g) for g in range(H)]
         y_bank = [ps.tile([P, 4, E], F32, name="y%d" % b) for b in range(4)]
-        sumsq = [sb.tile([P, CHUNK_STEPS], F32, name="sumsq%d" % c) for c in range(CHUNKS)]
-        rstd = [sb.tile([P, CHUNK_STEPS], F32, name="rstd%d" % c) for c in range(CHUNKS)]
-        squares = sb.tile([P, E], F32, name="squares")
-        t_words = t_sb[:, 0:PACK].unsqueeze(1).to_broadcast([P, P, PACK])
+        norm_groups = [list(range(8)), [8, 9, 12, 13], [10, 11, 14, 15]]
+        sumsq = [sb.tile([P, 8], F32, name="sumsq%d" % n) for n in range(3)]
+        rstd = [sb.tile([P, 8], F32, name="rstd%d" % n) for n in range(3)]
+        squares = [sb.tile([P, E], F32, name="squares%d" % n) for n in range(4)]
+
+        def norm_place(i):
+            for n in range(3):
+                if i in norm_groups[n]:
+                    return n, norm_groups[n].index(i)
+        t_words = t_sb[:, 0:PACK].unsqueeze(1).to_broadcast([P, 2 * P, PACK])
         probs = {}
         w_bf = {}
+        w_mx = {}
 
         def y_of(i):
             c, rest = divmod(i, CHUNK_STEPS)
-            return y_bank[2 * c + rest % 2][:, rest // 2, :]
+            m, g = divmod(rest, H)
+            if c == 0:
+                return y_bank[m][:, g, :]
+            return y_bank[2 + g // 2][:, 2 * (g % 2) + m, :]
 
-        def scores(i):
+        def scores(i, r):
             c, rest = divmod(i, CHUNK_STEPS)
             m, g = divmod(rest, H)
             rows = slice(ROWS * g, ROWS * (g + 1))
             q_codes, q_scales = q_mx[c]
             q_cols = slice(P * m, P * (m + 1))
-            for r in range(PACK):
-                k_codes, k_scales = k_mx[r // 2]
-                k_cols = slice(P * (r % 2), P * (r % 2 + 1))
-                nc.tensor.matmul_mx(
-                    out=score_bank[g][:, r, :],
-                    lhsT=k_codes[rows, k_cols].bitcast(FP8X4),
-                    lhsT_scale=k_scales[rows, k_cols],
-                    rhs=q_codes[rows, q_cols].bitcast(FP8X4),
-                    rhs_scale=q_scales[rows, q_cols],
-                    start=True,
-                    stop=True,
-                )
-
-        def sigmoid(i):
-            probs[i] = sb.tile([P, P, PACK], F32, name="probs%d" % i)
-            nc.scalar.activation(
-                out=probs[i][:], in_=score_bank[i % H][:].rearrange("p r n -> p n r"), func=ACT.Sigmoid
+            k_codes, k_scales = k_mx[r // 2]
+            k_cols = slice(P * (r % 2), P * (r % 2 + 1))
+            nc.tensor.matmul_mx(
+                out=score_bank[g][:, r, :],
+                lhsT=k_codes[rows, k_cols].bitcast(FP8X4),
+                lhsT_scale=k_scales[rows, k_cols],
+                rhs=q_codes[rows, q_cols].bitcast(FP8X4),
+                rhs_scale=q_scales[rows, q_cols],
+                start=True,
+                stop=True,
             )
 
-        def weigh(i):
-            w_bf[i] = sb.tile([P, P, PACK], BF16, name="w_bf%d" % i, align_bytes=64)
-            nc.vector.tensor_tensor(out=w_bf[i][:], in0=probs[i][:], in1=t_words, op=ALU.mult)
+        def sigmoid(i):
+            if i % 2 == 0:
+                probs[i // 2] = sb.tile([P, 2 * P, PACK], F32, name="probs%d" % i)
+            half = slice(P * (i % 2), P * (i % 2 + 1))
+            nc.scalar.activation(
+                out=probs[i // 2][:, half, :],
+                in_=score_bank[i % H][:].rearrange("p r n -> p n r"),
+                func=ACT.Sigmoid,
+            )
+
+        def weigh(a):
+            w_bf[a] = sb.tile([P, 2 * P, PACK], BF16, name="w_bf%d" % a, align_bytes=64)
+            nc.vector.tensor_tensor(out=w_bf[a][:], in0=probs[a][:], in1=t_words, op=ALU.mult)
+
+        def quantize_weights(a):
+            w_mx[a] = quantize("w%d" % a, w_bf[a][:].rearrange("p n r -> p (n r)"))
 
         def values(i):
-            w_codes, w_scales = quantize("w%d" % i, w_bf[i][:].rearrange("p n r -> p (n r)"))
+            w_codes, w_scales = w_mx[i // 2]
+            half = slice(P * (i % 2), P * (i % 2 + 1))
             nc.tensor.matmul_mx(
                 out=y_of(i),
-                lhsT=w_codes[:].bitcast(FP8X4),
-                lhsT_scale=w_scales[:],
+                lhsT=w_codes[:, half].bitcast(FP8X4),
+                lhsT_scale=w_scales[:, half],
                 rhs=v_codes[:].bitcast(FP8X4),
                 rhs_scale=v_scales[:],
                 start=True,
@@ -143,55 +160,79 @@ def tile_rows_a_sigmoid_onorm_kernel(tc, qT, kT, t, v, gn, out):
             )
 
         def sum_squares(i):
-            c, rest = divmod(i, CHUNK_STEPS)
+            n, col = norm_place(i)
             nc.scalar.activation(
-                out=squares[:], in_=y_of(i), func=ACT.Square, accum_out=sumsq[c][:, rest : rest + 1]
+                out=squares[i % 4][:], in_=y_of(i), func=ACT.Square, accum_out=sumsq[n][:, col : col + 1]
             )
 
-        def inverse_rms(c):
+        def inverse_rms(n):
+            cols = slice(0, len(norm_groups[n]))
             nc.scalar.activation(
-                out=rstd[c][:], in_=sumsq[c][:], func=ACT.Abs_reciprocal_sqrt, scale=1.0 / E, bias=256 * 1e-5
+                out=rstd[n][:, cols],
+                in_=sumsq[n][:, cols],
+                func=ACT.Abs_reciprocal_sqrt,
+                scale=1.0 / E,
+                bias=256 * 1e-5,
             )
 
-        def normalise_and_store(c):
-            for pair in range(H // 2):
-                result = sb.tile([P, 2, BLOCKS, E], F32, name="result%d_%d" % (c, pair))
-                for hh in range(2):
-                    for m in range(BLOCKS):
-                        rest = H * m + 2 * pair + hh
-                        nc.vector.scalar_tensor_tensor(
-                            out=result[:, hh, m, :],
-                            in0=y_of(CHUNK_STEPS * c + rest),
-                            scalar=rstd[c][:, rest : rest + 1],
-                            in1=gn_sb[:],
-                            op0=ALU.mult,
-                            op1=ALU.mult,
-                        )
-                dst = out[2 * pair : 2 * pair + 2, CHUNK_Q * c : CHUNK_Q * (c + 1), :]
-                nc.sync.dma_start(
-                    out=dst.rearrange("h (s m) e -> s h (m e)", m=BLOCKS),
-                    in_=result[:].rearrange("p h m e -> p h (m e)"),
-                )
+        def normalise_and_store(c, pair):
+            result = sb.tile([P, 2, BLOCKS, E], F32, name="result%d_%d" % (c, pair))
+            for hh in range(2):
+                for m in range(BLOCKS):
+                    i = CHUNK_STEPS * c + H * m + 2 * pair + hh
+                    n, col = norm_place(i)
+                    nc.vector.scalar_tensor_tensor(
+                        out=result[:, hh, m, :],
+                        in0=y_of(i),
+                        scalar=rstd[n][:, col : col + 1],
+                        in1=gn_sb[:],
+                        op0=ALU.mult,
+                        op1=ALU.mult,
+                    )
+            dst = out[2 * pair : 2 * pair + 2, CHUNK_Q * c : CHUNK_Q * (c + 1), :]
+            nc.sync.dma_start(
+                out=dst.rearrange("h (s m) e -> s h (m e)", m=BLOCKS),
+                in_=result[:].rearrange("p h m e -> p h (m e)"),
+            )
 
-        for i in range(H):
-            scores(i)
-        for i in range(STEPS + MULT_LAG + 1):
-            if i < STEPS:
-                sigmoid(i)
-                if i >= SQUARE_LAG:
-                    sum_squares(i - SQUARE_LAG)
+        for first in (0, 2):
+            for r in range(PACK):
+                scores(first, r)
+                scores(first + 1, r)
+        for i in range(STEPS):
+            sigmoid(i)
+            for r in range(2):
                 if i + H < STEPS:
-                    scores(i + H)
-            if i == STEPS:
-                inverse_rms(0)
-            if MULT_LAG <= i < STEPS + MULT_LAG:
-                weigh(i - MULT_LAG)
-            if i == MULT_LAG:
-                q_mx.append(quantize_queries(1))
-            if i > MULT_LAG:
-                values(i - MULT_LAG - 1)
-        for i in range(STEPS - SQUARE_LAG, STEPS):
-            sum_squares(i)
-        normalise_and_store(0)
-        inverse_rms(1)
-        normalise_and_store(1)
+                    scores(i + H, r)
+                if H <= i + H - 1 < STEPS:
+                    scores(i + H - 1, r + 2)
+            if i % 2 == 1:
+                a = i // 2
+                weigh(a)
+                if a == 0:
+                    q_mx.append(quantize_queries(1))
+                else:
+                    quantize_weights(a - 1)
+            if i == 7:
+                for j in range(0, 4):
+                    values(j)
+            if i == 9:
+                for j in range(0, 4):
+                    sum_squares(j)
+            if i == 12:
+                for j in range(4, 10):
+                    values(j)
+            if i == 13:
+                for j in range(4, 8):
+                    sum_squares(j)
+        inverse_rms(0)
+        quantize_weights(STEPS // 2 - 1)
+        for j in range(10, STEPS):
+            values(j)
+        for n in (1, 2):
+            for j in norm_groups[n]:
+                sum_squares(j)
+            inverse_rms(n)
+        for c in range(CHUNKS):
+            for pair in range(2):
+                normalise_and_store(c, pair)

@@ -21,8 +21,7 @@ CHUNK_Q = NQ // CHUNKS
 BLOCKS = CHUNK_Q // P
 STEPS = CHUNKS * BLOCKS * H
 CHUNK_STEPS = BLOCKS * H
-MULT_LAG = 2
-SQUARE_LAG = 5
+Q_WIDTHS = (128, 128, 256)
 
 
 def tile_rows_a_sigmoid_onorm_kernel(tc, qT, kT, t, v, gn, out):
@@ -45,14 +44,15 @@ def tile_rows_a_sigmoid_onorm_kernel(tc, qT, kT, t, v, gn, out):
             queue = nc.sync if g < 2 else nc.scalar
             queue.dma_start(out=k_raw[ROWS * g : ROWS * (g + 1)], in_=k_rows)
         q_rows = qT.rearrange("h (p j) n -> (h p) j n", j=PACK)
-        q_raw = [sb.tile([P, PACK, CHUNK_Q], F32, name="q_raw%d" % c) for c in range(CHUNKS)]
-        nc.sync.dma_start(out=q_raw[0][:], in_=q_rows[:, :, 0:CHUNK_Q])
-        v_raw = sb.tile([P, PACK, E], F32, name="v_raw")
-        nc.sync.dma_start(out=v_raw[:], in_=v[0].rearrange("(p j) e -> p j e", j=PACK))
+        q_raw = [sb.tile([P, PACK, w], F32, name="q_raw%d" % c) for c, w in enumerate(Q_WIDTHS)]
         t_sb = sb.tile([P, PACK], F32, name="t_sb")
-        nc.sync.dma_start(out=t_sb[:], in_=t.rearrange("(p j) o -> p (j o)", j=PACK))
-        nc.sync.dma_start(out=q_raw[1][:], in_=q_rows[:, :, CHUNK_Q:NQ])
+        v_raw = sb.tile([P, PACK, E], F32, name="v_raw")
         gn_sb = sb.tile([P, E], F32, name="gn_sb")
+        nc.sync.dma_start(out=q_raw[0][:], in_=q_rows[:, :, 0:P])
+        nc.sync.dma_start(out=q_raw[1][:], in_=q_rows[:, :, P : 2 * P])
+        nc.sync.dma_start(out=t_sb[:], in_=t.rearrange("(p j) o -> p (j o)", j=PACK))
+        nc.sync.dma_start(out=q_raw[2][:], in_=q_rows[:, :, 2 * P : NQ])
+        nc.sync.dma_start(out=v_raw[:], in_=v[0].rearrange("(p j) e -> p j e", j=PACK))
         nc.sync.dma_start(out=gn_sb[:], in_=gn)
 
         warm_in = sb.tile([P, 8], F32, name="warm_in")
@@ -65,38 +65,38 @@ def tile_rows_a_sigmoid_onorm_kernel(tc, qT, kT, t, v, gn, out):
         nc.vector.tensor_copy(out=k_bf[0][:].rearrange("p r s j -> p s j r"), in_=k_dealt[:, :, :, 0:2])
         nc.scalar.copy(out=k_bf[1][:].rearrange("p r s j -> p s j r"), in_=k_dealt[:, :, :, 2:4])
 
-        q_bf = [sb.tile([P, BLOCKS, P, PACK], BF16, name="q_bf%d" % c, align_bytes=64) for c in range(CHUNKS)]
+        q_bf = [sb.tile([P, w * PACK], BF16, name="q_bf%d" % c, align_bytes=64) for c, w in enumerate(Q_WIDTHS)]
+        v_bf = sb.tile([P, E * PACK], BF16, name="v_bf", align_bytes=64)
 
-        def cast_queries(c):
-            nc.vector.tensor_copy(
-                out=q_bf[c][:].rearrange("p m s j -> p s j m"),
-                in_=q_raw[c][:].rearrange("p j (s m) -> p s j m", m=BLOCKS),
+        def interleave(copy, dst, src):
+            copy(
+                out=dst[:].rearrange("p (c i j) -> p c j i", i=4, j=PACK),
+                in_=src[:].rearrange("p j (c i) -> p c j i", i=4),
             )
 
-        def quantize_queries(c):
-            return quantize("q%d" % c, q_bf[c][:].rearrange("p m s j -> p (m s j)"))
-
-        cast_queries(0)
+        interleave(nc.vector.tensor_copy, q_bf[0], q_raw[0])
+        interleave(nc.scalar.copy, q_bf[1], q_raw[1])
         k_mx = [quantize("k0", k_bf[0][:].rearrange("p r s j -> p (r s j)"))]
-        q_mx = [quantize_queries(0)]
+        q_mx = [quantize("q0", q_bf[0][:])]
         k_mx.append(quantize("k1", k_bf[1][:].rearrange("p r s j -> p (r s j)")))
-        v_bf = sb.tile([P, E, PACK], BF16, name="v_bf", align_bytes=64)
+        q_mx.append(quantize("q1", q_bf[1][:]))
         nc.vector.tensor_copy(
-            out=v_bf[:].rearrange("p (c i) j -> p c j i", i=4),
-            in_=v_raw[:].rearrange("p j (c i) -> p c j i", i=4),
+            out=q_bf[2][:].rearrange("p (m s j) -> p s j m", m=2, j=PACK),
+            in_=q_raw[2][:].rearrange("p j (s m) -> p s j m", m=2),
         )
-        cast_queries(1)
-        v_codes, v_scales = quantize("v", v_bf[:].rearrange("p e j -> p (e j)"))
+        interleave(nc.vector.tensor_copy, v_bf, v_raw)
+        q_mx.append(quantize("q2", q_bf[2][:]))
+        v_codes, v_scales = quantize("v", v_bf[:])
 
         score_bank = [ps.tile([P, PACK, P], F32, name="score%d" % g) for g in range(H)]
         y_bank = [ps.tile([P, 4, E], F32, name="y%d" % b) for b in range(4)]
-        norm_groups = [list(range(8)), [8, 9, 12, 13], [10, 11, 14, 15]]
-        sumsq = [sb.tile([P, 8], F32, name="sumsq%d" % n) for n in range(3)]
-        rstd = [sb.tile([P, 8], F32, name="rstd%d" % n) for n in range(3)]
+        norm_groups = [[0, 1, 2, 3], [4, 5, 6, 7], [8, 12, 9, 13], [10, 14, 11, 15]]
+        sumsq = [sb.tile([P, 8], F32, name="sumsq%d" % n) for n in range(4)]
+        rstd = [sb.tile([P, 8], F32, name="rstd%d" % n) for n in range(4)]
         squares = [sb.tile([P, E], F32, name="squares%d" % n) for n in range(4)]
 
         def norm_place(i):
-            for n in range(3):
+            for n in range(4):
                 if i in norm_groups[n]:
                     return n, norm_groups[n].index(i)
         t_words = t_sb[:, 0:PACK].unsqueeze(1).to_broadcast([P, 2 * P, PACK])
@@ -115,8 +115,8 @@ def tile_rows_a_sigmoid_onorm_kernel(tc, qT, kT, t, v, gn, out):
             c, rest = divmod(i, CHUNK_STEPS)
             m, g = divmod(rest, H)
             rows = slice(ROWS * g, ROWS * (g + 1))
-            q_codes, q_scales = q_mx[c]
-            q_cols = slice(P * m, P * (m + 1))
+            q_codes, q_scales = q_mx[m] if c == 0 else q_mx[2]
+            q_cols = slice(0, P) if c == 0 else slice(P * m, P * (m + 1))
             k_codes, k_scales = k_mx[r // 2]
             k_cols = slice(P * (r % 2), P * (r % 2 + 1))
             nc.tensor.matmul_mx(
@@ -162,7 +162,7 @@ def tile_rows_a_sigmoid_onorm_kernel(tc, qT, kT, t, v, gn, out):
         def sum_squares(i):
             n, col = norm_place(i)
             nc.scalar.activation(
-                out=squares[i % 4][:], in_=y_of(i), func=ACT.Square, accum_out=sumsq[n][:, col : col + 1]
+                out=squares[col][:], in_=y_of(i), func=ACT.Square, accum_out=sumsq[n][:, col : col + 1]
             )
 
         def inverse_rms(n):
@@ -175,28 +175,25 @@ def tile_rows_a_sigmoid_onorm_kernel(tc, qT, kT, t, v, gn, out):
                 bias=256 * 1e-5,
             )
 
-        def normalise_and_store(c, pair):
-            result = sb.tile([P, 2, BLOCKS, E], F32, name="result%d_%d" % (c, pair))
-            for hh in range(2):
-                for m in range(BLOCKS):
-                    i = CHUNK_STEPS * c + H * m + 2 * pair + hh
-                    n, col = norm_place(i)
-                    nc.vector.scalar_tensor_tensor(
-                        out=result[:, hh, m, :],
-                        in0=y_of(i),
-                        scalar=rstd[n][:, col : col + 1],
-                        in1=gn_sb[:],
-                        op0=ALU.mult,
-                        op1=ALU.mult,
-                    )
-            dst = out[2 * pair : 2 * pair + 2, CHUNK_Q * c : CHUNK_Q * (c + 1), :]
-            nc.sync.dma_start(
-                out=dst.rearrange("h (s m) e -> s h (m e)", m=BLOCKS),
-                in_=result[:].rearrange("p h m e -> p h (m e)"),
-            )
+        def normalise_and_store(steps, dst):
+            result = sb.tile([P, len(steps) * E], F32, name="result%d" % steps[0])
+            for place, i in enumerate(steps):
+                n, col = norm_place(i)
+                nc.vector.scalar_tensor_tensor(
+                    out=result[:, E * place : E * (place + 1)],
+                    in0=y_of(i),
+                    scalar=rstd[n][:, col : col + 1],
+                    in1=gn_sb[:],
+                    op0=ALU.mult,
+                    op1=ALU.mult,
+                )
+            nc.sync.dma_start(out=dst, in_=result[:].rearrange("p (h x) -> p h x", h=dst.shape[1]))
 
+        for r in range(2):
+            for g in range(H):
+                scores(g, r)
         for first in (0, 2):
-            for r in range(PACK):
+            for r in (2, 3):
                 scores(first, r)
                 scores(first + 1, r)
         for i in range(STEPS):
@@ -209,30 +206,18 @@ def tile_rows_a_sigmoid_onorm_kernel(tc, qT, kT, t, v, gn, out):
             if i % 2 == 1:
                 a = i // 2
                 weigh(a)
-                if a == 0:
-                    q_mx.append(quantize_queries(1))
-                else:
+                if a > 0:
                     quantize_weights(a - 1)
-            if i == 7:
-                for j in range(0, 4):
-                    values(j)
-            if i == 9:
-                for j in range(0, 4):
-                    sum_squares(j)
-            if i == 12:
-                for j in range(4, 10):
-                    values(j)
-            if i == 13:
-                for j in range(4, 8):
-                    sum_squares(j)
-        inverse_rms(0)
         quantize_weights(STEPS // 2 - 1)
-        for j in range(10, STEPS):
+        for j in range(STEPS):
             values(j)
-        for n in (1, 2):
+        for n in range(4):
             for j in norm_groups[n]:
                 sum_squares(j)
             inverse_rms(n)
-        for c in range(CHUNKS):
-            for pair in range(2):
-                normalise_and_store(c, pair)
+        for b in range(2):
+            normalise_and_store(norm_groups[b], out[:, P * b : P * (b + 1), :].rearrange("h s e -> s h e"))
+        late = out[:, 2 * P : NQ, :].rearrange("h (s m) e -> s h (m e)", m=2)
+        normalise_and_store(norm_groups[2], late[:, 0:2, :])
+        normalise_and_store(norm_groups[3][0:2], late[:, 2:3, :])
+        normalise_and_store(norm_groups[3][2:4], late[:, 3:4, :])

@@ -38,16 +38,16 @@ def tile_rows_a_sigmoid_onorm_kernel(tc, qT, kT, t, v, gn, out):
             nc.vector.quantize_mx(out=codes[:].bitcast(FP8X4), scales=scales[:], in_=values)
             return codes, scales
 
-        k_raw = sb.tile([P, PACK, N], F32, name="k_raw")
+        k_raw = sb.tile([P, PACK, N], F32, name="k_raw", align_bytes=256)
         k_rows = kT[0].rearrange("(p j) n -> p j n", j=PACK)
         for g in range(H):
             queue = nc.sync if g < 2 else nc.scalar
-            queue.dma_start(out=k_raw[ROWS * g : ROWS * (g + 1)], in_=k_rows)
+            queue.dma_start(out=k_raw[ROWS * g : ROWS * (g + 1)], in_=k_rows, max_dma_last_dim=4 * N)
         q_rows = qT.rearrange("h (p j) n -> (h p) j n", j=PACK)
-        q_raw = [sb.tile([P, PACK, w], F32, name="q_raw%d" % c) for c, w in enumerate(Q_WIDTHS)]
+        q_raw = [sb.tile([P, PACK, w], F32, name="q_raw%d" % c, align_bytes=256) for c, w in enumerate(Q_WIDTHS)]
         t_sb = sb.tile([P, PACK], F32, name="t_sb")
-        v_raw = sb.tile([P, PACK, E], F32, name="v_raw")
-        gn_sb = sb.tile([P, E], F32, name="gn_sb")
+        v_raw = sb.tile([P, PACK, E], F32, name="v_raw", align_bytes=256)
+        gn_sb = sb.tile([P, E], F32, name="gn_sb", align_bytes=256)
         nc.sync.dma_start(out=q_raw[0][:], in_=q_rows[:, :, 0:P])
         nc.sync.dma_start(out=q_raw[1][:], in_=q_rows[:, :, P : 2 * P])
         nc.sync.dma_start(out=t_sb[:], in_=t.rearrange("(p j) o -> p (j o)", j=PACK))
@@ -90,13 +90,13 @@ def tile_rows_a_sigmoid_onorm_kernel(tc, qT, kT, t, v, gn, out):
 
         score_bank = [ps.tile([P, PACK, P], F32, name="score%d" % g) for g in range(H)]
         y_bank = [ps.tile([P, 4, E], F32, name="y%d" % b) for b in range(4)]
-        norm_groups = [[0, 1, 2, 3], [4, 5, 6, 7], [8, 12, 9, 13], [10, 14, 11, 15]]
-        sumsq = [sb.tile([P, 8], F32, name="sumsq%d" % n) for n in range(4)]
-        rstd = [sb.tile([P, 8], F32, name="rstd%d" % n) for n in range(4)]
+        norm_groups = [[0, 1, 2, 3], [4, 5, 6, 7], [8, 12, 9, 13], [10, 14], [11, 15]]
+        sumsq = [sb.tile([P, 8], F32, name="sumsq%d" % n) for n in range(5)]
+        rstd = [sb.tile([P, 8], F32, name="rstd%d" % n) for n in range(5)]
         squares = [sb.tile([P, E], F32, name="squares%d" % n) for n in range(4)]
 
         def norm_place(i):
-            for n in range(4):
+            for n in range(5):
                 if i in norm_groups[n]:
                     return n, norm_groups[n].index(i)
         t_words = t_sb[:, 0:PACK].unsqueeze(1).to_broadcast([P, 2 * P, PACK])
@@ -176,7 +176,7 @@ def tile_rows_a_sigmoid_onorm_kernel(tc, qT, kT, t, v, gn, out):
             )
 
         def normalise_and_store(steps, dst):
-            result = sb.tile([P, len(steps) * E], F32, name="result%d" % steps[0])
+            result = sb.tile([P, len(steps) * E], F32, name="result%d" % steps[0], align_bytes=256)
             for place, i in enumerate(steps):
                 n, col = norm_place(i)
                 nc.vector.scalar_tensor_tensor(
@@ -208,16 +208,27 @@ def tile_rows_a_sigmoid_onorm_kernel(tc, qT, kT, t, v, gn, out):
                 weigh(a)
                 if a > 0:
                     quantize_weights(a - 1)
-        quantize_weights(STEPS // 2 - 1)
-        for j in range(STEPS):
-            values(j)
-        for n in range(4):
+
+        def norm(n):
             for j in norm_groups[n]:
                 sum_squares(j)
             inverse_rms(n)
-        for b in range(2):
-            normalise_and_store(norm_groups[b], out[:, P * b : P * (b + 1), :].rearrange("h s e -> s h e"))
+
+        def finish_early_block(b):
+            dst = out[:, P * b : P * (b + 1), :].rearrange("h s e -> s h e")
+            for first in (0, 2):
+                normalise_and_store(norm_groups[b][first : first + 2], dst[:, first : first + 2, :])
+
         late = out[:, 2 * P : NQ, :].rearrange("h (s m) e -> s h (m e)", m=2)
-        normalise_and_store(norm_groups[2], late[:, 0:2, :])
-        normalise_and_store(norm_groups[3][0:2], late[:, 2:3, :])
-        normalise_and_store(norm_groups[3][2:4], late[:, 3:4, :])
+        for j in range(STEPS - 2):
+            values(j)
+        norm(0)
+        finish_early_block(0)
+        quantize_weights(STEPS // 2 - 1)
+        for j in range(STEPS - 2, STEPS):
+            values(j)
+        for n in range(1, 5):
+            norm(n)
+        finish_early_block(1)
+        for g in range(H):
+            normalise_and_store([8 + g, 12 + g], late[:, g : g + 1, :])

from contextlib import ExitStack

import concourse.mybir as mybir

F32 = mybir.dt.float32
BF16 = mybir.dt.bfloat16
U32 = mybir.dt.uint32
U8 = mybir.dt.uint8
FP8X4 = mybir.dt.float8_e4m3fn_x4
ACT = mybir.ActivationFunctionType
ALU = mybir.AluOpType

H, D, NQ, N, E = 4, 128, 512, 512, 128
FLOPS = 2 * H * N * NQ * D + 2 * H * NQ * N * E

P = 128
PACK = 4
ROWS = D // PACK
CHUNKS = 2
CHUNK_Q = NQ // CHUNKS
BLOCKS = CHUNK_Q // P
STEPS = CHUNKS * BLOCKS * H
CHUNK_STEPS = BLOCKS * H
Q_WIDTHS = (128, 128, 256)


def tile_rows_a_sigmoid_onorm_kernel(tc, qT, kT, t, v, gn, out):
    nc = tc.nc
    with ExitStack() as ctx:
        sb = ctx.enter_context(tc.tile_pool(name="sb", bufs=1))
        ps = ctx.enter_context(tc.psum_pool(name="ps", bufs=1))
        ctx.enter_context(tc.manual_schedule())

        def quantize(name, values):
            words = values.shape[1] // PACK
            codes = sb.tile([P, words], U32, name=name + "_codes", align_bytes=64)
            scales = sb.tile([P, words], U8, name=name + "_scales", align_bytes=64)
            nc.vector.quantize_mx(out=codes[:].bitcast(FP8X4), scales=scales[:], in_=values)
            return codes, scales

        k_raw = sb.tile([P, PACK, N], F32, name="k_raw", align_bytes=256)
        k_rows = kT[0].rearrange("(p j) n -> p j n", j=PACK)
        for g in range(H):
            queue = nc.sync if g < 2 else nc.scalar
            queue.dma_start(out=k_raw[ROWS * g : ROWS * (g + 1)], in_=k_rows, max_dma_last_dim=4 * N)
        q_rows = qT.rearrange("h (p j) n -> (h p) j n", j=PACK)
        q_raw = [sb.tile([P, PACK, w], F32, name="q_raw%d" % c, align_bytes=256) for c, w in enumerate(Q_WIDTHS)]
        t_sb = sb.tile([P, PACK], F32, name="t_sb")
        v_raw = sb.tile([P, PACK, E], F32, name="v_raw", align_bytes=256)
        gn_sb = sb.tile([P, E], F32, name="gn_sb", align_bytes=256)
        nc.sync.dma_start(out=q_raw[0][:], in_=q_rows[:, :, 0:P])
        nc.sync.dma_start(out=q_raw[1][:], in_=q_rows[:, :, P : 2 * P])
        nc.sync.dma_start(out=t_sb[:], in_=t.rearrange("(p j) o -> p (j o)", j=PACK))
        nc.sync.dma_start(out=q_raw[2][:], in_=q_rows[:, :, 2 * P : NQ])
        nc.sync.dma_start(out=v_raw[:], in_=v[0].rearrange("(p j) e -> p j e", j=PACK))
        nc.sync.dma_start(out=gn_sb[:], in_=gn)

        warm_in = sb.tile([P, 8], F32, name="warm_in")
        warm_out = sb.tile([P, 8], F32, name="warm_out")
        nc.gpsimd.memset(warm_in[:], 0.0)
        nc.scalar.activation(out=warm_out[:], in_=warm_in[:], func=ACT.Sigmoid)

        k_dealt = k_raw[:].rearrange("p j (s r) -> p s j r", r=PACK)
        k_bf = [sb.tile([P, 2, P, PACK], BF16, name="k_bf%d" % a, align_bytes=64) for a in range(2)]
        nc.vector.tensor_copy(out=k_bf[0][:].rearrange("p r s j -> p s j r"), in_=k_dealt[:, :, :, 0:2])
        nc.scalar.copy(out=k_bf[1][:].rearrange("p r s j -> p s j r"), in_=k_dealt[:, :, :, 2:4])

        q_bf = [sb.tile([P, w * PACK], BF16, name="q_bf%d" % c, align_bytes=64) for c, w in enumerate(Q_WIDTHS)]
        v_bf = sb.tile([P, E * PACK], BF16, name="v_bf", align_bytes=64)

        def interleave(copy, dst, src):
            copy(
                out=dst[:].rearrange("p (c i j) -> p c j i", i=4, j=PACK),
                in_=src[:].rearrange("p j (c i) -> p c j i", i=4),
            )

        interleave(nc.vector.tensor_copy, q_bf[0], q_raw[0])
        interleave(nc.scalar.copy, q_bf[1], q_raw[1])
        k_mx = [quantize("k0", k_bf[0][:].rearrange("p r s j -> p (r s j)"))]
        q_mx = [quantize("q0", q_bf[0][:])]
        k_mx.append(quantize("k1", k_bf[1][:].rearrange("p r s j -> p (r s j)")))
        q_mx.append(quantize("q1", q_bf[1][:]))
        nc.vector.tensor_copy(
            out=q_bf[2][:].rearrange("p (m s j) -> p s j m", m=2, j=PACK),
            in_=q_raw[2][:].rearrange("p j (s m) -> p s j m", m=2),
        )
        interleave(nc.vector.tensor_copy, v_bf, v_raw)
        q_mx.append(quantize("q2", q_bf[2][:]))
        v_codes, v_scales = quantize("v", v_bf[:])

        score_bank = [ps.tile([P, PACK, P], F32, name="score%d" % g) for g in range(H)]
        y_bank = [ps.tile([P, 4, E], F32, name="y%d" % b) for b in range(4)]
        norm_groups = [[0, 1, 2, 3], [4, 5, 6, 7], [8, 12, 9, 13], [10, 14], [11, 15]]
        sumsq = [sb.tile([P, 8], F32, name="sumsq%d" % n) for n in range(5)]
        rstd = [sb.tile([P, 8], F32, name="rstd%d" % n) for n in range(5)]
        squares = [sb.tile([P, E], F32, name="squares%d" % n) for n in range(4)]

        def norm_place(i):
            for n in range(5):
                if i in norm_groups[n]:
                    return n, norm_groups[n].index(i)
        t_words = t_sb[:, 0:PACK].unsqueeze(1).to_broadcast([P, 2 * P, PACK])
        probs = {}
        w_bf = {}
        w_mx = {}

        def y_of(i):
            c, rest = divmod(i, CHUNK_STEPS)
            m, g = divmod(rest, H)
            if c == 0:
                return y_bank[m][:, g, :]
            return y_bank[2 + g // 2][:, 2 * (g % 2) + m, :]

        def scores(i, r):
            c, rest = divmod(i, CHUNK_STEPS)
            m, g = divmod(rest, H)
            rows = slice(ROWS * g, ROWS * (g + 1))
            q_codes, q_scales = q_mx[m] if c == 0 else q_mx[2]
            q_cols = slice(0, P) if c == 0 else slice(P * m, P * (m + 1))
            k_codes, k_scales = k_mx[r // 2]
            k_cols = slice(P * (r % 2), P * (r % 2 + 1))
            nc.tensor.matmul_mx(
                out=score_bank[g][:, r, :],
                lhsT=k_codes[rows, k_cols].bitcast(FP8X4),
                lhsT_scale=k_scales[rows, k_cols],
                rhs=q_codes[rows, q_cols].bitcast(FP8X4),
                rhs_scale=q_scales[rows, q_cols],
                start=True,
                stop=True,
            )

        def sigmoid(i):
            if i % 2 == 0:
                probs[i // 2] = sb.tile([P, 2 * P, PACK], F32, name="probs%d" % i)
            half = slice(P * (i % 2), P * (i % 2 + 1))
            nc.scalar.activation(
                out=probs[i // 2][:, half, :],
                in_=score_bank[i % H][:].rearrange("p r n -> p n r"),
                func=ACT.Sigmoid,
            )

        def weigh(a):
            w_bf[a] = sb.tile([P, 2 * P, PACK], BF16, name="w_bf%d" % a, align_bytes=64)
            nc.vector.tensor_tensor(out=w_bf[a][:], in0=probs[a][:], in1=t_words, op=ALU.mult)

        def quantize_weights(a):
            w_mx[a] = quantize("w%d" % a, w_bf[a][:].rearrange("p n r -> p (n r)"))

        def values(i):
            w_codes, w_scales = w_mx[i // 2]
            half = slice(P * (i % 2), P * (i % 2 + 1))
            nc.tensor.matmul_mx(
                out=y_of(i),
                lhsT=w_codes[:, half].bitcast(FP8X4),
                lhsT_scale=w_scales[:, half],
                rhs=v_codes[:].bitcast(FP8X4),
                rhs_scale=v_scales[:],
                start=True,
                stop=True,
            )

        def sum_squares(i):
            n, col = norm_place(i)
            nc.scalar.activation(
                out=squares[col][:], in_=y_of(i), func=ACT.Square, accum_out=sumsq[n][:, col : col + 1]
            )

        def inverse_rms(n):
            cols = slice(0, len(norm_groups[n]))
            nc.scalar.activation(
                out=rstd[n][:, cols],
                in_=sumsq[n][:, cols],
                func=ACT.Abs_reciprocal_sqrt,
                scale=1.0 / E,
                bias=256 * 1e-5,
            )

        def normalise_and_store(steps, dst):
            result = sb.tile([P, len(steps) * E], F32, name="result%d" % steps[0], align_bytes=256)
            for place, i in enumerate(steps):
                n, col = norm_place(i)
                nc.vector.scalar_tensor_tensor(
                    out=result[:, E * place : E * (place + 1)],
                    in0=y_of(i),
                    scalar=rstd[n][:, col : col + 1],
                    in1=gn_sb[:],
                    op0=ALU.mult,
                    op1=ALU.mult,
                )
            nc.sync.dma_start(out=dst, in_=result[:].rearrange("p (h x) -> p h x", h=dst.shape[1]))

        for r in range(2):
            for g in range(H):
                scores(g, r)
        for first in (0, 2):
            for r in (2, 3):
                scores(first, r)
                scores(first + 1, r)
        for i in range(STEPS):
            sigmoid(i)
            for r in range(2):
                if i + H < STEPS:
                    scores(i + H, r)
                if H <= i + H - 1 < STEPS:
                    scores(i + H - 1, r + 2)
            if i % 2 == 1:
                a = i // 2
                weigh(a)
                if a > 0:
                    quantize_weights(a - 1)

        def norm(n):
            for j in norm_groups[n]:
                sum_squares(j)
            inverse_rms(n)

        def finish_early_block(b):
            dst = out[:, P * b : P * (b + 1), :].rearrange("h s e -> s h e")
            for first in (0, 2):
                normalise_and_store(norm_groups[b][first : first + 2], dst[:, first : first + 2, :])

        late = out[:, 2 * P : NQ, :].rearrange("h (s m) e -> s h (m e)", m=2)
        for j in range(STEPS - 2):
            values(j)
        norm(0)
        finish_early_block(0)
        quantize_weights(STEPS // 2 - 1)
        for j in range(STEPS - 2, STEPS):
            values(j)
        for n in range(1, 5):
            norm(n)
        finish_early_block(1)
        for g in range(H):
            normalise_and_store([8 + g, 12 + g], late[:, g : g + 1, :])
